import numpy as np
import ml_dtypes


def mxq(x, axis, fmt="e4m3"):
    dtype, down = {"e4m3": (ml_dtypes.float8_e4m3fn, 7), "e5m2": (ml_dtypes.float8_e5m2, 14)}[fmt]
    v = np.moveaxis(np.asarray(x, np.float32).astype(ml_dtypes.bfloat16).astype(np.float64), axis, -1)
    blocks = v.reshape(v.shape[:-1] + (-1, 32))
    amax = np.abs(blocks).max(-1, keepdims=True)
    byte = np.maximum(np.where(amax > 0, np.frexp(amax)[1] - 1 + 127, 0) - down, 1)
    scale = np.exp2(byte - 127.0)
    codes = (blocks / scale).astype(np.float32).astype(dtype).astype(np.float64)
    return np.moveaxis((codes * scale).reshape(v.shape), -1, axis)


WIDE = False


def mx_kscale(k):
    if not WIDE:
        return np.ones(k)
    levels = np.array([10, -10, 5, -5, 0])
    if k % 512:
        return np.exp2(np.random.permutation(np.resize(levels, k // 32))).repeat(32)
    a = np.empty((k // 512, 16))
    for p in range(k // 512):
        a[p, :8] = np.random.permutation(np.resize(levels, 8))
        for g in range(8):
            far = levels[np.abs(levels - a[p, g]) >= 10]
            a[p, g + 8] = far[np.random.randint(len(far))]
    return np.exp2(a.ravel()).repeat(32)


def f64(x):
    return np.asarray(x).astype(np.float64)


def striped(idx):
    return np.tile(idx.reshape(-1, 16).T, (8, 1)).astype(np.uint16)


def unstriped(offs):
    return offs[:16].T.reshape(-1).astype(np.int64)


E2M1 = np.array([0.0, 0.5, 1.0, 1.5, 2.0, 3.0, 4.0, 6.0, -0.0, -0.5, -1.0, -1.5, -2.0, -3.0, -4.0, -6.0])


def pack_weight(w, fmt):
    k, n = w.shape
    w = f64(np.asarray(w, np.float32).astype(ml_dtypes.bfloat16)).reshape(k // 32, 32, n)
    amax = np.abs(w).max(1)
    if fmt == "e4m3":
        byte = np.frexp(amax)[1] - 1 + 127 - 7
    else:
        mant, ex = np.frexp(amax / 6.0)
        byte = np.where(mant > 0.5, ex, ex - 1) + 127
    byte = np.clip(np.where(amax > 0, byte, 1), 1, 254)
    scaled = (w * np.exp2(127.0 - byte)[:, None, :]).reshape(k, n).astype(np.float32)
    by_word = np.ascontiguousarray(scaled.reshape(k // 512, 128, 4, n).transpose(0, 1, 3, 2))
    if fmt == "e4m3":
        words = by_word.astype(ml_dtypes.float8_e4m3fn).view(np.uint8)
    else:
        c = by_word.astype(ml_dtypes.float4_e2m1fn).view(np.uint8) & 0xF
        words = (c[..., 0::2] | (c[..., 1::2] << 4)).reshape(k // 512, 128, 2 * n)
    return np.ascontiguousarray(words), np.ascontiguousarray(byte.astype(np.uint8).reshape(k // 512, 16, n))


def unpack_weight(words, scales, fmt):
    g, _, n = scales.shape
    words = np.ascontiguousarray(words).reshape(g, 128, n, -1)
    if fmt == "e4m3":
        vals = words.view(ml_dtypes.float8_e4m3fn).astype(np.float64)
    else:
        nib = np.empty((g, 128, n, 4), np.uint8)
        nib[..., 0::2] = words & 0xF
        nib[..., 1::2] = words >> 4
        vals = E2M1[nib]
    vals = vals * np.repeat(np.exp2(scales.astype(np.float64) - 127.0), 8, axis=1)[..., None]
    return vals.transpose(0, 1, 3, 2).reshape(g * 512, n)


def pack_table4(v):
    words, scales = pack_weight(v, "e2m1")
    g, t = words.shape[0] // 2, v.shape[1]
    words = words.reshape(g, 2, 128, t, 2).transpose(0, 2, 3, 1, 4)
    return np.concatenate([words.reshape(g, -1), scales.reshape(g, -1)], axis=1)


def unpack_table4(tab):
    g, t = tab.shape[0], tab.shape[1] // 544
    words = tab[:, :512 * t].reshape(g, 128, t, 2, 2).transpose(0, 3, 1, 2, 4).reshape(2 * g, 128, 2 * t)
    return unpack_weight(words, tab[:, 512 * t:].reshape(2 * g, 16, t), "e2m1")


def gelu(v):
    return 0.5 * v * (1.0 + np.tanh(np.sqrt(2.0 / np.pi) * (v + 0.044715 * v**3)))


K, M, T, S = 3072, 1024, 2048, 1024


def setup_inputs():
    n = np.random.standard_normal
    s = mx_kscale(K)[:, None]
    return {
        "tab": pack_table4(n((K, T)) * s),
        "w": (n((K, M)) / np.sqrt(K) / s).astype(np.float32),
        "b": (0.3 * n(1024)).astype(np.float32),
        "offs": striped(np.random.permutation(T)[:S]),
    }


def reference(tab, w, b, offs):
    tab_ = unpack_table4(tab)[:, unstriped(offs)]
    w_ = mxq(f64(w), 0, "e4m3")
    y = tab_.T @ w_
    return gelu(y + f64(b)[None, :])

@@ -1,0 +1,247 @@
+from contextlib import ExitStack
+
+import concourse.mybir as mybir
+from concourse.masks import make_identity
+
+K, M, T, S = 3072, 1024, 2048, 1024
+FLOPS = 2 * K * M * S
+
+F32 = mybir.dt.float32
+BF16 = mybir.dt.bfloat16
+I32 = mybir.dt.int32
+U32 = mybir.dt.uint32
+U16 = mybir.dt.uint16
+U8 = mybir.dt.uint8
+FP8X4 = mybir.dt.float8_e4m3fn_x4
+FP4X4 = mybir.dt.float4_e2m1fn_x4
+GELU = mybir.ActivationFunctionType.Gelu_apprx_tanh
+ADD = mybir.AluOpType.add
+
+P = 128
+PACK = 4
+K_PASS = P * PACK
+PASSES = K // K_PASS
+PAIRS = PASSES // 2
+N_TILE = 512
+HALVES = M // N_TILE
+TILES = S // P
+MOVED_ROWS = 112
+
+
+def tile_list_tab4_tm_gelu_kernel(tc, tab, w, b, offs, out):
+    nc = tc.nc
+    with ExitStack() as ctx:
+        keep = ctx.enter_context(tc.tile_pool(name="keep", bufs=1))
+        ring = ctx.enter_context(tc.tile_pool(name="ring", bufs=1))
+        shared = ctx.enter_context(tc.tile_pool(name="shared", bufs=1))
+        psum = ctx.enter_context(tc.psum_pool(name="psum", bufs=1))
+
+        offsets = keep.tile([P, S // 16], U16, name="offsets")
+        nc.sync.dma_start(offsets[:], offs)
+
+        scale_win = []
+        for h in range(2):
+            win = shared.tile([P, T // 4], I32, name="scale_win%d" % h, align_bytes=64, offset=2048 * h)
+            nc.vector.memset(win[:], 0)
+            scale_win.append(win)
+        moved = keep.tile([P, PAIRS - 1, 2 * S // 4], I32, name="moved", align_bytes=64)
+        nc.vector.memset(moved[:], 0)
+
+        tab_scales = tab[:, 512 * T : 544 * T].rearrange("m (h q t) -> m h q t", h=2, q=16)
+        for h in range(2):
+            for quad in range(4):
+                nc.gpsimd.dma_start(
+                    out=scale_win[h][32 * quad : 32 * quad + 4 * PAIRS, :],
+                    in_=tab_scales[:, h, 4 * quad : 4 * quad + 4, :].bitcast(I32),
+                )
+        b_rows = keep.tile([P, M // P], F32, name="b_rows")
+        nc.sync.dma_start(out=b_rows[:], in_=b.rearrange("(p c) -> p c", p=P))
+
+        warm = keep.tile([P, 1], F32, name="warm")
+        nc.vector.memset(warm[:], 0.0)
+        nc.scalar.activation(out=warm[:], in_=warm[:], func=GELU)
+
+        word_win = {}
+        raw = {}
+
+        def load_words(m):
+            win = keep.tile([P, T], U32, name="word_win%d" % m, align_bytes=64)
+            nc.sync.dma_start(
+                out=win[:].bitcast(I32),
+                in_=tab[m, 0 : 512 * T].rearrange("(p c) -> p c", p=P).bitcast(I32),
+            )
+            word_win[m] = win
+
+        def load_w(half, a):
+            rows = w[a * K_PASS : (a + 1) * K_PASS, half * N_TILE : (half + 1) * N_TILE]
+            tile = ring.tile([P, PACK, N_TILE], F32, name="raw", bufs=8)
+            nc.sync.dma_start(out=tile[:], in_=rows.rearrange("(p j) n -> p j n", j=PACK))
+            raw[half, a] = tile
+
+        load_words(0)
+        load_w(0, 0)
+        load_w(0, 1)
+        load_words(1)
+        load_w(0, 2)
+        load_w(0, 3)
+        load_words(2)
+        for a in range(4, PASSES):
+            load_w(0, a)
+
+        ident = keep.tile([P, P], F32, name="ident")
+        make_identity(nc, ident[:])
+        bias = keep.tile([P, P, M // P], F32, name="bias")
+        for g in range(2):
+            spread = psum.tile([P, 4, P], F32, name="bank%d" % (TILES - 2 + g))
+            for c in range(4):
+                col = 4 * g + c
+                nc.tensor.transpose(spread[:, c, :], b_rows[:, col : col + 1].to_broadcast([P, P]), ident[:])
+            nc.scalar.copy(out=bias[:, :, 4 * g : 4 * g + 4], in_=spread[:].rearrange("q c p -> q p c"))
+        bias_row = bias[:].rearrange("q p c -> q (p c)")
+
+        picked_scales = keep.tile([P, 2, S], U8, name="picked_scales", align_bytes=64)
+        parted = {}
+
+        def gather_scales(h):
+            nc.vector.tensor_copy(picked_scales[:, h, :], scale_win[h][:].bitcast(U8).indirect(offsets[:]))
+
+        def gather_words(m):
+            if m == 0:
+                picked = keep.tile([P, S], U32, name="picked0", align_bytes=64)
+            else:
+                picked = shared.tile([P, S], U32, name="picked", align_bytes=64, offset=3072)
+            nc.vector.tensor_copy(picked[:], word_win[m][:].indirect(offsets[:]))
+            return picked
+
+        def part_words(m, picked):
+            tile = keep.tile([P, 2, 2 * S], U8, name="parted%d" % m, align_bytes=64)
+            nc.vector.tensor_copy(
+                out=tile[:].bitcast(U16),
+                in_=picked[:].bitcast(U16).rearrange("p (j h) -> p h j", h=2),
+            )
+            parted[m] = tile
+
+        def move_scales(m):
+            src = picked_scales[:].rearrange("p h j -> p (h j)").bitcast(I32)
+            nc.gpsimd.dma_start(out=moved[0:MOVED_ROWS, m - 1, :], in_=src[4 * m : 4 * m + MOVED_ROWS, :])
+
+        def table_plane(a, cols):
+            m, h = divmod(a, 2)
+            if m == 0:
+                return picked_scales[:, h, cols]
+            return moved[:, m - 1, :].bitcast(U8).rearrange("p (h j) -> p h j", h=2)[:, h, cols]
+
+        grouped = {}
+        codes = {}
+        planes = {}
+
+        def cast_w(half, a, scalar_cols):
+            if half == 1 and a % 2 == 1:
+                tile = shared.tile([P, N_TILE, PACK], BF16, name="grouped_late", align_bytes=64, offset=7168)
+            else:
+                tile = ring.tile([P, N_TILE, PACK], BF16, name="grouped%d" % (a % 2), align_bytes=64)
+            src = raw[half, a]
+            for copy, cols in ((nc.scalar.copy, slice(0, scalar_cols)), (nc.vector.tensor_copy, slice(scalar_cols, N_TILE))):
+                if cols.start < cols.stop:
+                    copy(
+                        out=tile[:, cols, :].rearrange("p (c i) t -> p c t i", i=4),
+                        in_=src[:, :, cols].rearrange("p t (c i) -> p c t i", i=4),
+                    )
+            grouped[half, a] = tile
+
+        def quantize_w(half, a):
+            code_at = {(0, 0): 0, (0, 4): 7168, (0, 5): 9216}.get((half, a))
+            plane_at = {(0, 1): 2048, (0, 2): 2560, (0, 5): 11264, (1, 0): 11264}.get((half, a))
+            code_pool = keep if code_at is None else shared
+            plane_pool = keep if plane_at is None else shared
+            code = code_pool.tile([P, N_TILE], U32, name="codes%d_%d" % (half, a), align_bytes=64, offset=code_at)
+            plane = plane_pool.tile([P, N_TILE], U8, name="plane%d_%d" % (half, a), align_bytes=64, offset=plane_at)
+            nc.vector.quantize_mx(
+                out=code[:].bitcast(FP8X4),
+                scales=plane[:],
+                in_=grouped[half, a][:].rearrange("p n j -> p (n j)"),
+            )
+            codes[half, a] = code
+            planes[half, a] = plane
+
+        acc = {}
+
+        def multiply(half, a, i):
+            if a == 0:
+                acc[half, i] = psum.tile([P, N_TILE], F32, name="bank%d" % i)
+            m, h = divmod(a, 2)
+            nc.tensor.matmul_mx(
+                out=acc[half, i][:],
+                lhsT=parted[m][:, h, 2 * P * i : 2 * P * (i + 1)].bitcast(FP4X4),
+                lhsT_scale=table_plane(a, slice(P * i, P * (i + 1))),
+                rhs=codes[half, a][:].bitcast(FP8X4),
+                rhs_scale=planes[half, a][:],
+                start=(a == 0),
+                stop=(a == PASSES - 1),
+            )
+
+        result = {}
+
+        def add_bias(half, i):
+            tile = keep.tile([P, N_TILE], F32, name="result%d_%d" % (half, i))
+            nc.vector.tensor_tensor(
+                out=tile[:], in0=acc[half, i][:], in1=bias_row[:, half * N_TILE : (half + 1) * N_TILE], op=ADD
+            )
+            result[half, i] = tile
+
+        def activate(half, i):
+            tile = result[half, i]
+            nc.scalar.activation(out=tile[:], in_=tile[:], func=GELU)
+
+        def store(half, i):
+            nc.sync.dma_start(
+                out=out[P * i : P * (i + 1), half * N_TILE : (half + 1) * N_TILE], in_=result[half, i][:]
+            )
+
+        part_words(0, gather_words(0))
+        gather_scales(0)
+        cast_w(0, 0, N_TILE)
+        quantize_w(0, 0)
+        gather_scales(1)
+        for m in range(1, PAIRS):
+            move_scales(m)
+        for a in range(PASSES):
+            if a in (2, 4):
+                part_words(a // 2, gather_words(a // 2))
+            if a > 0:
+                cast_w(0, a, N_TILE if a < PASSES - 1 else N_TILE // 2)
+                quantize_w(0, a)
+            for i in range(TILES):
+                multiply(0, a, i)
+            load_w(1, a)
+
+        for i in range(TILES):
+            add_bias(0, i)
+            activate(0, i)
+            if i == 1:
+                cast_w(1, 0, N_TILE // 2)
+            if i == 2:
+                quantize_w(1, 0)
+            if i == 4:
+                cast_w(1, 1, N_TILE // 2)
+            if i == 5:
+                quantize_w(1, 1)
+        for i in range(TILES + 4):
+            if i < TILES:
+                multiply(1, 0, i)
+            if i >= 4:
+                multiply(1, 1, i - 4)
+        for a in range(2, PASSES):
+            cast_w(1, a, N_TILE // 2)
+            quantize_w(1, a)
+            if a < PASSES - 2:
+                for i in range(TILES):
+                    multiply(1, a, i)
+        for i in range(TILES):
+            store(0, i)
+        for i in range(TILES):
+            multiply(1, PASSES - 2, i)
+            multiply(1, PASSES - 1, i)
+            add_bias(1, i)
+            activate(1, i)
+            store(1, i)

@@ -25,121 +25,78 @@ PAIRS = PASSES // 2
 N_TILE = 512
 HALVES = M // N_TILE
 TILES = S // P
-MOVED_ROWS = 112
+KIB = 1024
+
+SLOT = 8 * KIB
+LATE_LOADS = 12
+SCALAR_COLS = {(0, 5): 256, (1, 2): 192, (1, 3): 192, (1, 4): 192, (1, 5): 192}
 
 
 def tile_list_tab4_tm_gelu_kernel(tc, tab, w, b, offs, out):
     nc = tc.nc
     with ExitStack() as ctx:
         keep = ctx.enter_context(tc.tile_pool(name="keep", bufs=1))
-        ring = ctx.enter_context(tc.tile_pool(name="ring", bufs=1))
+        ring = ctx.enter_context(tc.tile_pool(name="ring", bufs=2))
         shared = ctx.enter_context(tc.tile_pool(name="shared", bufs=1))
+        behind = ctx.enter_context(tc.tile_pool(name="behind", bufs=1))
         psum = ctx.enter_context(tc.psum_pool(name="psum", bufs=1))
-
-        offsets = keep.tile([P, S // 16], U16, name="offsets")
-        nc.sync.dma_start(offsets[:], offs)
-
-        scale_win = []
-        for h in range(2):
-            win = shared.tile([P, T // 4], I32, name="scale_win%d" % h, align_bytes=64, offset=2048 * h)
-            nc.vector.memset(win[:], 0)
-            scale_win.append(win)
-        moved = keep.tile([P, PAIRS - 1, 2 * S // 4], I32, name="moved", align_bytes=64)
-        nc.vector.memset(moved[:], 0)
-
-        tab_scales = tab[:, 512 * T : 544 * T].rearrange("m (h q t) -> m h q t", h=2, q=16)
-        for h in range(2):
-            for quad in range(4):
-                nc.gpsimd.dma_start(
-                    out=scale_win[h][32 * quad : 32 * quad + 4 * PAIRS, :],
-                    in_=tab_scales[:, h, 4 * quad : 4 * quad + 4, :].bitcast(I32),
-                )
-        b_rows = keep.tile([P, M // P], F32, name="b_rows")
-        nc.sync.dma_start(out=b_rows[:], in_=b.rearrange("(p c) -> p c", p=P))
-
-        warm = keep.tile([P, 1], F32, name="warm")
-        nc.vector.memset(warm[:], 0.0)
-        nc.scalar.activation(out=warm[:], in_=warm[:], func=GELU)
 
         word_win = {}
         raw = {}
+        picked = {}
+        parted = {}
+        grouped = {}
+        codes = {}
+        planes = {}
+        acc = {}
+        result = {}
 
-        def load_words(m):
-            win = keep.tile([P, T], U32, name="word_win%d" % m, align_bytes=64)
+        taken = []
+
+        def landing(shape, dtype, name, late):
+            if late:
+                taken.append(name)
+                return behind.tile(shape, dtype, name=name, align_bytes=64, offset=SLOT * (len(taken) - 1))
+            return keep.tile(shape, dtype, name=name, align_bytes=64)
+
+        def load_words(m, late=True):
+            win = landing([P, T], U32, "word_win%d" % m, late)
             nc.sync.dma_start(
                 out=win[:].bitcast(I32),
                 in_=tab[m, 0 : 512 * T].rearrange("(p c) -> p c", p=P).bitcast(I32),
             )
             word_win[m] = win
 
-        def load_w(half, a):
+        def load_w(half, a, late=True):
             rows = w[a * K_PASS : (a + 1) * K_PASS, half * N_TILE : (half + 1) * N_TILE]
-            tile = ring.tile([P, PACK, N_TILE], F32, name="raw", bufs=8)
+            tile = landing([P, PACK, N_TILE], F32, "raw%d_%d" % (half, a), late)
             nc.sync.dma_start(out=tile[:], in_=rows.rearrange("(p j) n -> p j n", j=PACK))
             raw[half, a] = tile
 
-        load_words(0)
-        load_w(0, 0)
-        load_w(0, 1)
-        load_words(1)
-        load_w(0, 2)
-        load_w(0, 3)
-        load_words(2)
-        for a in range(4, PASSES):
-            load_w(0, a)
-
-        ident = keep.tile([P, P], F32, name="ident")
-        make_identity(nc, ident[:])
-        bias = keep.tile([P, P, M // P], F32, name="bias")
-        for g in range(2):
-            spread = psum.tile([P, 4, P], F32, name="bank%d" % (TILES - 2 + g))
-            for c in range(4):
-                col = 4 * g + c
-                nc.tensor.transpose(spread[:, c, :], b_rows[:, col : col + 1].to_broadcast([P, P]), ident[:])
-            nc.scalar.copy(out=bias[:, :, 4 * g : 4 * g + 4], in_=spread[:].rearrange("q c p -> q p c"))
-        bias_row = bias[:].rearrange("q p c -> q (p c)")
-
-        picked_scales = keep.tile([P, 2, S], U8, name="picked_scales", align_bytes=64)
-        parted = {}
-
-        def gather_scales(h):
-            nc.vector.tensor_copy(picked_scales[:, h, :], scale_win[h][:].bitcast(U8).indirect(offsets[:]))
-
         def gather_words(m):
-            if m == 0:
-                picked = keep.tile([P, S], U32, name="picked0", align_bytes=64)
-            else:
-                picked = shared.tile([P, S], U32, name="picked", align_bytes=64, offset=3072)
-            nc.vector.tensor_copy(picked[:], word_win[m][:].indirect(offsets[:]))
-            return picked
+            tile = ring.tile([P, S], U32, name="picked", align_bytes=64)
+            nc.vector.tensor_copy(tile[:], word_win[m][:].indirect(offsets[:]))
+            picked[m] = tile
 
-        def part_words(m, picked):
+        def part_words(m):
             tile = keep.tile([P, 2, 2 * S], U8, name="parted%d" % m, align_bytes=64)
             nc.vector.tensor_copy(
                 out=tile[:].bitcast(U16),
-                in_=picked[:].bitcast(U16).rearrange("p (j h) -> p h j", h=2),
+                in_=picked[m][:].bitcast(U16).rearrange("p (j h) -> p h j", h=2),
             )
             parted[m] = tile
 
-        def move_scales(m):
-            src = picked_scales[:].rearrange("p h j -> p (h j)").bitcast(I32)
-            nc.gpsimd.dma_start(out=moved[0:MOVED_ROWS, m - 1, :], in_=src[4 * m : 4 * m + MOVED_ROWS, :])
+        def move_scales(a):
+            src = picked_scales[:].bitcast(I32)
+            for r in range(4):
+                nc.sync.dma_start(out=table_planes[r:P:32, a, :], in_=src[16 * a + r : 16 * (a + 1) : 4, :])
 
-        def table_plane(a, cols):
-            m, h = divmod(a, 2)
-            if m == 0:
-                return picked_scales[:, h, cols]
-            return moved[:, m - 1, :].bitcast(U8).rearrange("p (h j) -> p h j", h=2)[:, h, cols]
-
-        grouped = {}
-        codes = {}
-        planes = {}
-
-        def cast_w(half, a, scalar_cols):
-            if half == 1 and a % 2 == 1:
-                tile = shared.tile([P, N_TILE, PACK], BF16, name="grouped_late", align_bytes=64, offset=7168)
+        def cast_w(half, a):
+            scalar_cols = SCALAR_COLS.get((half, a), N_TILE)
+            if half == 1 and a in (2, 4):
+                tile = shared.tile([P, N_TILE, PACK], BF16, name="grouped_late", align_bytes=64, offset=0)
             else:
-                tile = ring.tile([P, N_TILE, PACK], BF16, name="grouped%d" % (a % 2), align_bytes=64)
+                tile = keep.tile([P, N_TILE, PACK], BF16, name="grouped%d" % ((a + half) % 2), align_bytes=64)
             src = raw[half, a]
             for copy, cols in ((nc.scalar.copy, slice(0, scalar_cols)), (nc.vector.tensor_copy, slice(scalar_cols, N_TILE))):
                 if cols.start < cols.stop:
@@ -150,12 +107,13 @@ def tile_list_tab4_tm_gelu_kernel(tc, tab, w, b, offs, out):
             grouped[half, a] = tile
 
         def quantize_w(half, a):
-            code_at = {(0, 0): 0, (0, 4): 7168, (0, 5): 9216}.get((half, a))
-            plane_at = {(0, 1): 2048, (0, 2): 2560, (0, 5): 11264, (1, 0): 11264}.get((half, a))
-            code_pool = keep if code_at is None else shared
-            plane_pool = keep if plane_at is None else shared
-            code = code_pool.tile([P, N_TILE], U32, name="codes%d_%d" % (half, a), align_bytes=64, offset=code_at)
-            plane = plane_pool.tile([P, N_TILE], U8, name="plane%d_%d" % (half, a), align_bytes=64, offset=plane_at)
+            if half == 0 and a >= PASSES - 2:
+                code = shared.tile(
+                    [P, N_TILE], U32, name="codes0_%d" % a, align_bytes=64, offset=2 * KIB * (a - PASSES + 2)
+                )
+            else:
+                code = keep.tile([P, N_TILE], U32, name="codes%d_%d" % (half, a), align_bytes=64)
+            plane = keep.tile([P, N_TILE], U8, name="plane%d_%d" % (half, a), align_bytes=64)
             nc.vector.quantize_mx(
                 out=code[:].bitcast(FP8X4),
                 scales=plane[:],
@@ -164,8 +122,6 @@ def tile_list_tab4_tm_gelu_kernel(tc, tab, w, b, offs, out):
             codes[half, a] = code
             planes[half, a] = plane
 
-        acc = {}
-
         def multiply(half, a, i):
             if a == 0:
                 acc[half, i] = psum.tile([P, N_TILE], F32, name="bank%d" % i)
@@ -173,14 +129,19 @@ def tile_list_tab4_tm_gelu_kernel(tc, tab, w, b, offs, out):
             nc.tensor.matmul_mx(
                 out=acc[half, i][:],
                 lhsT=parted[m][:, h, 2 * P * i : 2 * P * (i + 1)].bitcast(FP4X4),
-                lhsT_scale=table_plane(a, slice(P * i, P * (i + 1))),
+                lhsT_scale=table_planes[:, a, :].bitcast(U8)[:, P * i : P * (i + 1)],
                 rhs=codes[half, a][:].bitcast(FP8X4),
                 rhs_scale=planes[half, a][:],
                 start=(a == 0),
                 stop=(a == PASSES - 1),
             )
 
-        result = {}
+        def multiply_staggered(half, a):
+            for step in range(TILES + 4):
+                if step >= 4:
+                    multiply(half, a + 1, step - 4)
+                if step < TILES:
+                    multiply(half, a, step)
 
         def add_bias(half, i):
             tile = keep.tile([P, N_TILE], F32, name="result%d_%d" % (half, i))
@@ -198,50 +159,76 @@ def tile_list_tab4_tm_gelu_kernel(tc, tab, w, b, offs, out):
                 out=out[P * i : P * (i + 1), half * N_TILE : (half + 1) * N_TILE], in_=result[half, i][:]
             )
 
-        part_words(0, gather_words(0))
-        gather_scales(0)
-        cast_w(0, 0, N_TILE)
-        quantize_w(0, 0)
-        gather_scales(1)
-        for m in range(1, PAIRS):
-            move_scales(m)
+        offsets = keep.tile([P, S // 16], U16, name="offsets")
+        nc.sync.dma_start(offsets[:], offs)
+        early = behind.tile([P, LATE_LOADS * SLOT // 4], I32, name="early", align_bytes=64, offset=0)
+        scale_win = early[:, 0 : T // 4]
+        nc.vector.memset(scale_win[32 * PAIRS : P, :], 0)
+        for m in range(PAIRS):
+            nc.sync.dma_start(
+                out=scale_win[32 * m : 32 * (m + 1), :],
+                in_=tab[m, 512 * T : 544 * T].rearrange("(q t) -> q t", q=32).bitcast(I32),
+            )
+        load_words(0, late=False)
+        b_rows = keep.tile([P, M // P], F32, name="b_rows")
+        nc.sync.dma_start(out=b_rows[:], in_=b.rearrange("(p c) -> p c", p=P))
+        load_w(0, 0, late=False)
+        load_w(0, 1, late=False)
+
+        table_planes = keep.tile([P, PASSES, S // 4], I32, name="table_planes", align_bytes=64)
+        nc.vector.memset(table_planes[:], 0)
+        warm = keep.tile([P, 1], F32, name="warm")
+        nc.vector.memset(warm[:], 0.0)
+        nc.scalar.activation(out=warm[:], in_=warm[:], func=GELU)
+
+        picked_scales = keep.tile([P, S], U8, name="picked_scales", align_bytes=64)
+        nc.vector.tensor_copy(picked_scales[:], scale_win.bitcast(U8).indirect(offsets[:]))
+        later = [(load_words, 1), (load_w, 0, 2), (load_w, 0, 3), (load_words, 2), (load_w, 0, 4), (load_w, 0, 5)]
         for a in range(PASSES):
-            if a in (2, 4):
-                part_words(a // 2, gather_words(a // 2))
-            if a > 0:
-                cast_w(0, a, N_TILE if a < PASSES - 1 else N_TILE // 2)
-                quantize_w(0, a)
-            for i in range(TILES):
-                multiply(0, a, i)
+            move_scales(a)
+            later[a][0](*later[a][1:])
+        for a in range(PASSES):
             load_w(1, a)
+
+        for a in range(PASSES):
+            if a % 2 == 0:
+                gather_words(a // 2)
+                part_words(a // 2)
+            cast_w(0, a)
+            quantize_w(0, a)
+            if a == 0:
+                ident = keep.tile([P, P], F32, name="ident")
+                make_identity(nc, ident[:])
+                bias = keep.tile([P, P, M // P], F32, name="bias")
+                for g in range(2):
+                    spread = psum.tile([P, 4, P], F32, name="bank%d" % (TILES - 2 + g))
+                    for c in range(4):
+                        col = 4 * g + c
+                        nc.tensor.transpose(spread[:, c, :], b_rows[:, col : col + 1].to_broadcast([P, P]), ident[:])
+                    nc.scalar.copy(out=bias[:, :, 4 * g : 4 * g + 4], in_=spread[:].rearrange("q c p -> q p c"))
+                bias_row = bias[:].rearrange("q p c -> q (p c)")
+            if a < PASSES - 2:
+                for i in range(TILES):
+                    multiply(0, a, i)
+        multiply_staggered(0, PASSES - 2)
 
         for i in range(TILES):
             add_bias(0, i)
-            activate(0, i)
-            if i == 1:
-                cast_w(1, 0, N_TILE // 2)
-            if i == 2:
+            if i == 3:
+                cast_w(1, 0)
                 quantize_w(1, 0)
-            if i == 4:
-                cast_w(1, 1, N_TILE // 2)
-            if i == 5:
-                quantize_w(1, 1)
-        for i in range(TILES + 4):
-            if i < TILES:
-                multiply(1, 0, i)
-            if i >= 4:
-                multiply(1, 1, i - 4)
-        for a in range(2, PASSES):
-            cast_w(1, a, N_TILE // 2)
-            quantize_w(1, a)
+        for a in range(PASSES):
+            if a > 0:
+                cast_w(1, a)
+                quantize_w(1, a)
             if a < PASSES - 2:
                 for i in range(TILES):
                     multiply(1, a, i)
         for i in range(TILES):
+            activate(0, i)
             store(0, i)
+        multiply_staggered(1, PASSES - 2)
         for i in range(TILES):
-            multiply(1, PASSES - 2, i)
-            multiply(1, PASSES - 1, i)
             add_bias(1, i)
             activate(1, i)
             store(1, i)

@@ -28,8 +28,10 @@ TILES = S // P
 KIB = 1024
 
 SLOT = 8 * KIB
-LATE_LOADS = 12
-SCALAR_COLS = {(0, 5): 256, (1, 2): 192, (1, 3): 192, (1, 4): 192, (1, 5): 192}
+LATE_LOADS = 10
+MOVED_ROWS = 112
+SCALE_LOADS_ON_SYNC = 2
+SCALAR_COLS = {(0, 2): 192, (0, 3): 192, (0, 4): 192, (0, 5): 192, (1, 2): 192, (1, 3): 192, (1, 4): 192, (1, 5): 192}
 
 
 def tile_list_tab4_tm_gelu_kernel(tc, tab, w, b, offs, out):
@@ -87,9 +89,15 @@ def tile_list_tab4_tm_gelu_kernel(tc, tab, w, b, offs, out):
             parted[m] = tile
 
         def move_scales(a):
-            src = picked_scales[:].bitcast(I32)
-            for r in range(4):
-                nc.sync.dma_start(out=table_planes[r:P:32, a, :], in_=src[16 * a + r : 16 * (a + 1) : 4, :])
+            m, h = divmod(a, 2)
+            shift = 4 * (PAIRS * h + m)
+            rows = min(MOVED_ROWS, P - shift)
+            nc.sync.dma_start(
+                out=table_planes[0:rows, a - 1, :], in_=picked_scales[:].bitcast(I32)[shift : shift + rows, :]
+            )
+
+        def table_plane(a):
+            return picked_scales[:] if a == 0 else table_planes[:, a - 1, :].bitcast(U8)
 
         def cast_w(half, a):
             scalar_cols = SCALAR_COLS.get((half, a), N_TILE)
@@ -129,7 +137,7 @@ def tile_list_tab4_tm_gelu_kernel(tc, tab, w, b, offs, out):
             nc.tensor.matmul_mx(
                 out=acc[half, i][:],
                 lhsT=parted[m][:, h, 2 * P * i : 2 * P * (i + 1)].bitcast(FP4X4),
-                lhsT_scale=table_planes[:, a, :].bitcast(U8)[:, P * i : P * (i + 1)],
+                lhsT_scale=table_plane(a)[:, P * i : P * (i + 1)],
                 rhs=codes[half, a][:].bitcast(FP8X4),
                 rhs_scale=planes[half, a][:],
                 start=(a == 0),
@@ -163,39 +171,57 @@ def tile_list_tab4_tm_gelu_kernel(tc, tab, w, b, offs, out):
         nc.sync.dma_start(offsets[:], offs)
         early = behind.tile([P, LATE_LOADS * SLOT // 4], I32, name="early", align_bytes=64, offset=0)
         scale_win = early[:, 0 : T // 4]
-        nc.vector.memset(scale_win[32 * PAIRS : P, :], 0)
-        for m in range(PAIRS):
-            nc.sync.dma_start(
-                out=scale_win[32 * m : 32 * (m + 1), :],
-                in_=tab[m, 512 * T : 544 * T].rearrange("(q t) -> q t", q=32).bitcast(I32),
-            )
-        load_words(0, late=False)
-        b_rows = keep.tile([P, M // P], F32, name="b_rows")
-        nc.sync.dma_start(out=b_rows[:], in_=b.rearrange("(p c) -> p c", p=P))
-        load_w(0, 0, late=False)
-        load_w(0, 1, late=False)
-
-        table_planes = keep.tile([P, PASSES, S // 4], I32, name="table_planes", align_bytes=64)
-        nc.vector.memset(table_planes[:], 0)
         warm = keep.tile([P, 1], F32, name="warm")
         nc.vector.memset(warm[:], 0.0)
         nc.scalar.activation(out=warm[:], in_=warm[:], func=GELU)
+        nc.vector.memset(scale_win, 0)
+        tab_scales = tab[:, 512 * T : 544 * T].rearrange("m (h q t) -> m h q t", h=2, q=16)
 
+        load_words(0, late=False)
+        for piece in range(8):
+            h, quad = divmod(piece, 4)
+            first = 32 * quad + 4 * PAIRS * h
+            queue = nc.sync if piece < SCALE_LOADS_ON_SYNC else nc.scalar
+            queue.dma_start(
+                out=scale_win[first : first + 4 * PAIRS, :],
+                in_=tab_scales[:, h, 4 * quad : 4 * quad + 4, :].bitcast(I32),
+            )
+        load_w(0, 0, late=False)
+        load_words(1, late=False)
+        b_rows = keep.tile([P, M // P], F32, name="b_rows")
+        nc.sync.dma_start(out=b_rows[:], in_=b.rearrange("(p c) -> p c", p=P))
+        load_w(0, 1, late=False)
+        load_words(2, late=False)
+
+        table_planes = keep.tile([P, PASSES - 1, S // 4], I32, name="table_planes", align_bytes=64)
+        nc.vector.memset(table_planes[96:P, :, :], 0)
+
+        gather_words(0)
+        part_words(0)
         picked_scales = keep.tile([P, S], U8, name="picked_scales", align_bytes=64)
         nc.vector.tensor_copy(picked_scales[:], scale_win.bitcast(U8).indirect(offsets[:]))
-        later = [(load_words, 1), (load_w, 0, 2), (load_w, 0, 3), (load_words, 2), (load_w, 0, 4), (load_w, 0, 5)]
-        for a in range(PASSES):
-            move_scales(a)
-            later[a][0](*later[a][1:])
+        move_scales(1)
+        move_scales(2)
+        load_w(0, 2)
+        move_scales(3)
+        load_w(0, 3)
+        move_scales(4)
+        move_scales(5)
+        load_w(0, 4)
+        load_w(0, 5)
         for a in range(PASSES):
             load_w(1, a)
 
         for a in range(PASSES):
-            if a % 2 == 0:
-                gather_words(a // 2)
-                part_words(a // 2)
+            if a == 1:
+                gather_words(1)
+                part_words(1)
+            if a == 2:
+                gather_words(2)
             cast_w(0, a)
             quantize_w(0, a)
+            if a == 2:
+                part_words(2)
             if a == 0:
                 ident = keep.tile([P, P], F32, name="ident")
                 make_identity(nc, ident[:])

@@ -22,16 +22,18 @@ PACK = 4
 K_PASS = P * PACK
 PASSES = K // K_PASS
 PAIRS = PASSES // 2
+BLOCKS = K_PASS // 32
 N_TILE = 512
-HALVES = M // N_TILE
 TILES = S // P
-KIB = 1024
-
-SLOT = 8 * KIB
+WORD_BYTES = P * T * 4
+SLOT = 4 * PACK * N_TILE
 LATE_LOADS = 10
-MOVED_ROWS = 112
-SCALE_LOADS_ON_SYNC = 2
-SCALAR_COLS = {(0, 2): 192, (0, 3): 192, (0, 4): 192, (0, 5): 192, (1, 2): 192, (1, 3): 192, (1, 4): 192, (1, 5): 192}
+
+SCALAR_COLS = ((128, 512, 512, 512, 320, 192), (192, 512, 512, 128, 192, 128))
+FIRST_HELD_BANK = 5
+QUANTIZE_AFTER_ADD = {3: 0, FIRST_HELD_BANK - 1: 1}
+BANK_BYTES = 4 * N_TILE
+HELD_AT = LATE_LOADS * SLOT
 
 
 def tile_list_tab4_tm_gelu_kernel(tc, tab, w, b, offs, out):
@@ -39,222 +41,198 @@ def tile_list_tab4_tm_gelu_kernel(tc, tab, w, b, offs, out):
     with ExitStack() as ctx:
         keep = ctx.enter_context(tc.tile_pool(name="keep", bufs=1))
         ring = ctx.enter_context(tc.tile_pool(name="ring", bufs=2))
-        shared = ctx.enter_context(tc.tile_pool(name="shared", bufs=1))
-        behind = ctx.enter_context(tc.tile_pool(name="behind", bufs=1))
+        placed = ctx.enter_context(tc.tile_pool(name="placed", bufs=1))
         psum = ctx.enter_context(tc.psum_pool(name="psum", bufs=1))
 
-        word_win = {}
+        slot_of = {}
+        word_window = {}
         raw = {}
-        picked = {}
         parted = {}
-        grouped = {}
         codes = {}
-        planes = {}
+        w_plane = {}
         acc = {}
-        result = {}
-
-        taken = []
+        summed = {}
 
         def landing(shape, dtype, name, late):
-            if late:
-                taken.append(name)
-                return behind.tile(shape, dtype, name=name, align_bytes=64, offset=SLOT * (len(taken) - 1))
-            return keep.tile(shape, dtype, name=name, align_bytes=64)
+            if not late:
+                return keep.tile(shape, dtype, name=name, align_bytes=64)
+            slot_of[name] = len(slot_of)
+            return placed.tile(shape, dtype, name=name, align_bytes=64, offset=SLOT * slot_of[name])
 
-        def load_words(m, late=True):
-            win = landing([P, T], U32, "word_win%d" % m, late)
+        def load_words(m, late):
+            window = landing([P, T], U32, "word_window%d" % m, late)
             nc.sync.dma_start(
-                out=win[:].bitcast(I32),
-                in_=tab[m, 0 : 512 * T].rearrange("(p c) -> p c", p=P).bitcast(I32),
+                out=window[:].bitcast(I32),
+                in_=tab[m, 0:WORD_BYTES].rearrange("(p c) -> p c", p=P).bitcast(I32),
             )
-            word_win[m] = win
+            word_window[m] = window
 
-        def load_w(half, a, late=True):
+        def load_w(half, a, late):
             rows = w[a * K_PASS : (a + 1) * K_PASS, half * N_TILE : (half + 1) * N_TILE]
             tile = landing([P, PACK, N_TILE], F32, "raw%d_%d" % (half, a), late)
             nc.sync.dma_start(out=tile[:], in_=rows.rearrange("(p j) n -> p j n", j=PACK))
             raw[half, a] = tile
 
-        def gather_words(m):
-            tile = ring.tile([P, S], U32, name="picked", align_bytes=64)
-            nc.vector.tensor_copy(tile[:], word_win[m][:].indirect(offsets[:]))
-            picked[m] = tile
+        def move_scales(a):
+            rows = picked_scales[:].bitcast(I32)
+            for r in range(4):
+                nc.sync.dma_start(
+                    out=table_planes[r:P:32, a, :], in_=rows[BLOCKS * a + r : BLOCKS * (a + 1) : 4, :]
+                )
 
-        def part_words(m):
+        def gather_words(m):
+            picked = ring.tile([P, S], U32, name="picked", align_bytes=64)
+            nc.vector.tensor_copy(picked[:], word_window[m][:].indirect(offsets[:]))
             tile = keep.tile([P, 2, 2 * S], U8, name="parted%d" % m, align_bytes=64)
             nc.vector.tensor_copy(
                 out=tile[:].bitcast(U16),
-                in_=picked[m][:].bitcast(U16).rearrange("p (j h) -> p h j", h=2),
+                in_=picked[:].bitcast(U16).rearrange("p (j h) -> p h j", h=2),
             )
             parted[m] = tile
 
-        def move_scales(a):
-            m, h = divmod(a, 2)
-            shift = 4 * (PAIRS * h + m)
-            rows = min(MOVED_ROWS, P - shift)
-            nc.sync.dma_start(
-                out=table_planes[0:rows, a - 1, :], in_=picked_scales[:].bitcast(I32)[shift : shift + rows, :]
-            )
-
-        def table_plane(a):
-            return picked_scales[:] if a == 0 else table_planes[:, a - 1, :].bitcast(U8)
-
-        def cast_w(half, a):
-            scalar_cols = SCALAR_COLS.get((half, a), N_TILE)
-            if half == 1 and a in (2, 4):
-                tile = shared.tile([P, N_TILE, PACK], BF16, name="grouped_late", align_bytes=64, offset=0)
-            else:
-                tile = keep.tile([P, N_TILE, PACK], BF16, name="grouped%d" % ((a + half) % 2), align_bytes=64)
-            src = raw[half, a]
-            for copy, cols in ((nc.scalar.copy, slice(0, scalar_cols)), (nc.vector.tensor_copy, slice(scalar_cols, N_TILE))):
-                if cols.start < cols.stop:
-                    copy(
-                        out=tile[:, cols, :].rearrange("p (c i) t -> p c t i", i=4),
-                        in_=src[:, :, cols].rearrange("p t (c i) -> p c t i", i=4),
-                    )
-            grouped[half, a] = tile
-
         def quantize_w(half, a):
-            if half == 0 and a >= PASSES - 2:
-                code = shared.tile(
-                    [P, N_TILE], U32, name="codes0_%d" % a, align_bytes=64, offset=2 * KIB * (a - PASSES + 2)
+            if (half, a) == (1, 1):
+                grouped = placed.tile(
+                    [P, N_TILE, PACK], BF16, name="grouped_held", align_bytes=64, offset=HELD_AT + BANK_BYTES // 2
                 )
             else:
-                code = keep.tile([P, N_TILE], U32, name="codes%d_%d" % (half, a), align_bytes=64)
-            plane = keep.tile([P, N_TILE], U8, name="plane%d_%d" % (half, a), align_bytes=64)
+                grouped = ring.tile([P, N_TILE, PACK], BF16, name="grouped", align_bytes=64)
+            split = SCALAR_COLS[half][a]
+            for copy, cols in ((nc.scalar.copy, slice(0, split)), (nc.vector.tensor_copy, slice(split, N_TILE))):
+                if cols.start < cols.stop:
+                    copy(
+                        out=grouped[:, cols, :].rearrange("p (c i) t -> p c t i", i=4),
+                        in_=raw[half, a][:, :, cols].rearrange("p t (c i) -> p c t i", i=4),
+                    )
+            code = keep.tile([P, N_TILE], U32, name="codes%d_%d" % (half, a), align_bytes=64)
+            plane = keep.tile([P, N_TILE], U8, name="w_plane%d_%d" % (half, a), align_bytes=64)
             nc.vector.quantize_mx(
-                out=code[:].bitcast(FP8X4),
-                scales=plane[:],
-                in_=grouped[half, a][:].rearrange("p n j -> p (n j)"),
+                out=code[:].bitcast(FP8X4), scales=plane[:], in_=grouped[:].rearrange("p n t -> p (n t)")
             )
             codes[half, a] = code
-            planes[half, a] = plane
+            w_plane[half, a] = plane
 
-        def multiply(half, a, i):
-            if a == 0:
+        def multiply(half, a, i, stop=False):
+            start = (half, i) not in acc
+            if start:
                 acc[half, i] = psum.tile([P, N_TILE], F32, name="bank%d" % i)
             m, h = divmod(a, 2)
             nc.tensor.matmul_mx(
                 out=acc[half, i][:],
                 lhsT=parted[m][:, h, 2 * P * i : 2 * P * (i + 1)].bitcast(FP4X4),
-                lhsT_scale=table_plane(a)[:, P * i : P * (i + 1)],
+                lhsT_scale=table_planes[:, a, :].bitcast(U8)[:, P * i : P * (i + 1)],
                 rhs=codes[half, a][:].bitcast(FP8X4),
-                rhs_scale=planes[half, a][:],
-                start=(a == 0),
-                stop=(a == PASSES - 1),
+                rhs_scale=w_plane[half, a][:],
+                start=start,
+                stop=stop,
             )
 
-        def multiply_staggered(half, a):
-            for step in range(TILES + 4):
-                if step >= 4:
-                    multiply(half, a + 1, step - 4)
-                if step < TILES:
-                    multiply(half, a, step)
-
-        def add_bias(half, i):
-            tile = keep.tile([P, N_TILE], F32, name="result%d_%d" % (half, i))
+        def add_bias(half, i, cols):
+            if half == 0 and i >= FIRST_HELD_BANK:
+                at = HELD_AT + BANK_BYTES * (i - FIRST_HELD_BANK)
+                summed[half, i] = placed.tile([P, N_TILE], F32, name="held%d" % i, align_bytes=64, offset=at)
+            elif (half, i) not in summed:
+                summed[half, i] = keep.tile([P, N_TILE], F32, name="summed%d_%d" % (half, i))
             nc.vector.tensor_tensor(
-                out=tile[:], in0=acc[half, i][:], in1=bias_row[:, half * N_TILE : (half + 1) * N_TILE], op=ADD
+                out=summed[half, i][:, cols],
+                in0=acc[half, i][:, cols],
+                in1=bias_row[:, half * N_TILE : (half + 1) * N_TILE][:, cols],
+                op=ADD,
             )
-            result[half, i] = tile
 
-        def activate(half, i):
-            tile = result[half, i]
-            nc.scalar.activation(out=tile[:], in_=tile[:], func=GELU)
+        def activate_and_store(half, i, cols, result):
+            nc.scalar.activation(out=result[:, cols], in_=summed[half, i][:, cols], func=GELU)
+            rows = out[P * i : P * (i + 1), half * N_TILE : (half + 1) * N_TILE]
+            nc.sync.dma_start(out=rows[:, cols], in_=result[:, cols])
 
-        def store(half, i):
-            nc.sync.dma_start(
-                out=out[P * i : P * (i + 1), half * N_TILE : (half + 1) * N_TILE], in_=result[half, i][:]
-            )
+        whole = slice(0, N_TILE)
 
         offsets = keep.tile([P, S // 16], U16, name="offsets")
         nc.sync.dma_start(offsets[:], offs)
-        early = behind.tile([P, LATE_LOADS * SLOT // 4], I32, name="early", align_bytes=64, offset=0)
-        scale_win = early[:, 0 : T // 4]
+        span = placed.tile([P, LATE_LOADS * SLOT // 4], I32, name="span", align_bytes=64, offset=0)
+        scale_window = span[:, 0 : T // 4]
+        nc.vector.memset(scale_window[BLOCKS * PASSES : P, :], 0)
+        for m in range(PAIRS):
+            nc.sync.dma_start(
+                out=scale_window[2 * BLOCKS * m : 2 * BLOCKS * (m + 1), :],
+                in_=tab[m, WORD_BYTES : WORD_BYTES + 2 * BLOCKS * T]
+                .rearrange("(q t) -> q t", q=2 * BLOCKS)
+                .bitcast(I32),
+            )
+        load_w(0, 0, late=False)
+        b_rows = keep.tile([P, M // P], F32, name="b_rows")
+        nc.sync.dma_start(out=b_rows[:], in_=b.rearrange("(p c) -> p c", p=P))
+        load_words(0, late=False)
+        load_w(0, 1, late=False)
+        load_words(1, late=False)
+        load_w(0, 2, late=False)
+
+        table_planes = keep.tile([P, PASSES, S // 4], I32, name="table_planes", align_bytes=64)
+        nc.vector.memset(table_planes[:], 0)
         warm = keep.tile([P, 1], F32, name="warm")
         nc.vector.memset(warm[:], 0.0)
         nc.scalar.activation(out=warm[:], in_=warm[:], func=GELU)
-        nc.vector.memset(scale_win, 0)
-        tab_scales = tab[:, 512 * T : 544 * T].rearrange("m (h q t) -> m h q t", h=2, q=16)
 
-        load_words(0, late=False)
-        for piece in range(8):
-            h, quad = divmod(piece, 4)
-            first = 32 * quad + 4 * PAIRS * h
-            queue = nc.sync if piece < SCALE_LOADS_ON_SYNC else nc.scalar
-            queue.dma_start(
-                out=scale_win[first : first + 4 * PAIRS, :],
-                in_=tab_scales[:, h, 4 * quad : 4 * quad + 4, :].bitcast(I32),
-            )
-        load_w(0, 0, late=False)
-        load_words(1, late=False)
-        b_rows = keep.tile([P, M // P], F32, name="b_rows")
-        nc.sync.dma_start(out=b_rows[:], in_=b.rearrange("(p c) -> p c", p=P))
-        load_w(0, 1, late=False)
-        load_words(2, late=False)
-
-        table_planes = keep.tile([P, PASSES - 1, S // 4], I32, name="table_planes", align_bytes=64)
-        nc.vector.memset(table_planes[96:P, :, :], 0)
+        picked_scales = keep.tile([P, S], U8, name="picked_scales", align_bytes=64)
+        nc.vector.tensor_copy(picked_scales[:], scale_window.bitcast(U8).indirect(offsets[:]))
+        move_scales(0)
+        load_words(2, late=True)
+        late_w = [(0, a) for a in range(3, PASSES)] + [(1, a) for a in range(PASSES)]
+        for place, (half, a) in enumerate(late_w):
+            if place + 1 < PASSES:
+                move_scales(place + 1)
+            load_w(half, a, late=True)
 
         gather_words(0)
-        part_words(0)
-        picked_scales = keep.tile([P, S], U8, name="picked_scales", align_bytes=64)
-        nc.vector.tensor_copy(picked_scales[:], scale_win.bitcast(U8).indirect(offsets[:]))
-        move_scales(1)
-        move_scales(2)
-        load_w(0, 2)
-        move_scales(3)
-        load_w(0, 3)
-        move_scales(4)
-        move_scales(5)
-        load_w(0, 4)
-        load_w(0, 5)
-        for a in range(PASSES):
-            load_w(1, a)
+        quantize_w(0, 0)
+
+        ident = keep.tile([P, P], F32, name="ident")
+        make_identity(nc, ident[:])
+        bias = keep.tile([P, P, M // P], F32, name="bias")
+        for g in range(2):
+            spread = psum.tile([P, 4, P], F32, name="bank%d" % (TILES - 2 + g))
+            for c in range(4):
+                column = b_rows[:, 4 * g + c : 4 * g + c + 1]
+                nc.tensor.transpose(spread[:, c, :], column.to_broadcast([P, P]), ident[:])
+            nc.scalar.copy(out=bias[:, :, 4 * g : 4 * g + 4], in_=spread[:].rearrange("q c p -> q p c"))
+        bias_row = bias[:].rearrange("q p c -> q (p c)")
 
         for a in range(PASSES):
-            if a == 1:
-                gather_words(1)
-                part_words(1)
-            if a == 2:
-                gather_words(2)
-            cast_w(0, a)
-            quantize_w(0, a)
-            if a == 2:
-                part_words(2)
-            if a == 0:
-                ident = keep.tile([P, P], F32, name="ident")
-                make_identity(nc, ident[:])
-                bias = keep.tile([P, P, M // P], F32, name="bias")
-                for g in range(2):
-                    spread = psum.tile([P, 4, P], F32, name="bank%d" % (TILES - 2 + g))
-                    for c in range(4):
-                        col = 4 * g + c
-                        nc.tensor.transpose(spread[:, c, :], b_rows[:, col : col + 1].to_broadcast([P, P]), ident[:])
-                    nc.scalar.copy(out=bias[:, :, 4 * g : 4 * g + 4], in_=spread[:].rearrange("q c p -> q p c"))
-                bias_row = bias[:].rearrange("q p c -> q (p c)")
-            if a < PASSES - 2:
-                for i in range(TILES):
-                    multiply(0, a, i)
-        multiply_staggered(0, PASSES - 2)
-
-        for i in range(TILES):
-            add_bias(0, i)
-            if i == 3:
-                cast_w(1, 0)
-                quantize_w(1, 0)
-        for a in range(PASSES):
+            if a in (1, 3):
+                gather_words((a + 1) // 2)
             if a > 0:
-                cast_w(1, a)
-                quantize_w(1, a)
-            if a < PASSES - 2:
-                for i in range(TILES):
+                quantize_w(0, a)
+            for i in range(TILES):
+                multiply(0, a, i, stop=(a == PASSES - 1))
+
+        for i in range(TILES):
+            add_bias(0, i, whole)
+            if i in QUANTIZE_AFTER_ADD:
+                quantize_w(1, QUANTIZE_AFTER_ADD[i])
+        for a in (0, 1):
+            for i in range(FIRST_HELD_BANK):
+                multiply(1, a, i)
+        for i in range(FIRST_HELD_BANK, TILES):
+            multiply(1, 1, i)
+            multiply(1, 0, i)
+        for a in range(2, PASSES):
+            quantize_w(1, a)
+            if a < PASSES - 1:
+                for i in range(TILES if a < PASSES - 2 else TILES // 2):
                     multiply(1, a, i)
+
         for i in range(TILES):
-            activate(0, i)
-            store(0, i)
-        multiply_staggered(1, PASSES - 2)
-        for i in range(TILES):
-            add_bias(1, i)
-            activate(1, i)
-            store(1, i)
+            at = SLOT * slot_of["raw1_%d" % (1 + i // 4)] + BANK_BYTES * (i % 4)
+            result = placed.tile([P, N_TILE], F32, name="result%d" % i, align_bytes=64, offset=at)
+            activate_and_store(0, i, whole, result)
+
+        for i in range(TILES // 2):
+            upper = i + TILES // 2
+            multiply(1, PASSES - 1, i, stop=True)
+            multiply(1, PASSES - 1, upper)
+            multiply(1, PASSES - 2, upper, stop=True)
+            for done in (i, upper):
+                pieces = [whole] if done < TILES - 1 else [slice(0, N_TILE // 2), slice(N_TILE // 2, N_TILE)]
+                for cols in pieces:
+                    add_bias(1, done, cols)
+                    activate_and_store(1, done, cols, summed[1, done])

@@ -29,8 +29,8 @@ WORD_BYTES = P * T * 4
 SLOT = 4 * PACK * N_TILE
 LATE_LOADS = 10
 
-SCALAR_COLS = ((128, 512, 512, 512, 320, 192), (192, 512, 512, 128, 192, 128))
-FIRST_HELD_BANK = 5
+SCALAR_COLS = ((512, 512, 512, 384, 512, 320), (256, 512, 384, 128, 128, 192))
+FIRST_HELD_BANK = 6
 QUANTIZE_AFTER_ADD = {3: 0, FIRST_HELD_BANK - 1: 1}
 BANK_BYTES = 4 * N_TILE
 HELD_AT = LATE_LOADS * SLOT
@@ -73,12 +73,11 @@ def tile_list_tab4_tm_gelu_kernel(tc, tab, w, b, offs, out):
             nc.sync.dma_start(out=tile[:], in_=rows.rearrange("(p j) n -> p j n", j=PACK))
             raw[half, a] = tile
 
-        def move_scales(a):
-            rows = picked_scales[:].bitcast(I32)
+        def move_scales(m):
+            rows = picked_scales[:].rearrange("p h j -> p (h j)").bitcast(I32)
+            planes = table_planes[:, 2 * m : 2 * m + 2, :].rearrange("p h j -> p (h j)")
             for r in range(4):
-                nc.sync.dma_start(
-                    out=table_planes[r:P:32, a, :], in_=rows[BLOCKS * a + r : BLOCKS * (a + 1) : 4, :]
-                )
+                nc.sync.dma_start(out=planes[r:P:32, :], in_=rows[4 * r + m : 4 * BLOCKS : 16, :])
 
         def gather_words(m):
             picked = ring.tile([P, S], U32, name="picked", align_bytes=64)
@@ -92,9 +91,7 @@ def tile_list_tab4_tm_gelu_kernel(tc, tab, w, b, offs, out):
 
         def quantize_w(half, a):
             if (half, a) == (1, 1):
-                grouped = placed.tile(
-                    [P, N_TILE, PACK], BF16, name="grouped_held", align_bytes=64, offset=HELD_AT + BANK_BYTES // 2
-                )
+                grouped = placed.tile([P, N_TILE, PACK], BF16, name="grouped_held", align_bytes=64, offset=HELD_AT)
             else:
                 grouped = ring.tile([P, N_TILE, PACK], BF16, name="grouped", align_bytes=64)
             split = SCALAR_COLS[half][a]
@@ -150,19 +147,18 @@ def tile_list_tab4_tm_gelu_kernel(tc, tab, w, b, offs, out):
         offsets = keep.tile([P, S // 16], U16, name="offsets")
         nc.sync.dma_start(offsets[:], offs)
         span = placed.tile([P, LATE_LOADS * SLOT // 4], I32, name="span", align_bytes=64, offset=0)
-        scale_window = span[:, 0 : T // 4]
-        nc.vector.memset(scale_window[BLOCKS * PASSES : P, :], 0)
-        for m in range(PAIRS):
+        scale_windows = span[:, 0 : 2 * T // 4].rearrange("p (h t) -> p h t", h=2)
+        nc.vector.memset(scale_windows[4 * BLOCKS : P, :, :], 0)
+        for place in range(4):
+            scale_rows = tab[place % PAIRS, WORD_BYTES : WORD_BYTES + 2 * BLOCKS * T]
             nc.sync.dma_start(
-                out=scale_window[2 * BLOCKS * m : 2 * BLOCKS * (m + 1), :],
-                in_=tab[m, WORD_BYTES : WORD_BYTES + 2 * BLOCKS * T]
-                .rearrange("(q t) -> q t", q=2 * BLOCKS)
-                .bitcast(I32),
+                out=scale_windows[place : 4 * BLOCKS : 4, :, :],
+                in_=scale_rows.rearrange("(h q t) -> q h t", h=2, q=BLOCKS).bitcast(I32),
             )
-        load_w(0, 0, late=False)
+        load_words(0, late=False)
         b_rows = keep.tile([P, M // P], F32, name="b_rows")
         nc.sync.dma_start(out=b_rows[:], in_=b.rearrange("(p c) -> p c", p=P))
-        load_words(0, late=False)
+        load_w(0, 0, late=False)
         load_w(0, 1, late=False)
         load_words(1, late=False)
         load_w(0, 2, late=False)
@@ -173,15 +169,18 @@ def tile_list_tab4_tm_gelu_kernel(tc, tab, w, b, offs, out):
         nc.vector.memset(warm[:], 0.0)
         nc.scalar.activation(out=warm[:], in_=warm[:], func=GELU)
 
-        picked_scales = keep.tile([P, S], U8, name="picked_scales", align_bytes=64)
-        nc.vector.tensor_copy(picked_scales[:], scale_window.bitcast(U8).indirect(offsets[:]))
+        picked_scales = keep.tile([P, 2, S], U8, name="picked_scales", align_bytes=64)
+        for h in range(2):
+            nc.vector.tensor_copy(picked_scales[:, h, :], scale_windows[:, h, :].bitcast(U8).indirect(offsets[:]))
         move_scales(0)
+        load_w(0, 3, late=True)
         load_words(2, late=True)
-        late_w = [(0, a) for a in range(3, PASSES)] + [(1, a) for a in range(PASSES)]
-        for place, (half, a) in enumerate(late_w):
-            if place + 1 < PASSES:
-                move_scales(place + 1)
-            load_w(half, a, late=True)
+        move_scales(1)
+        load_w(0, 4, late=True)
+        load_w(0, 5, late=True)
+        move_scales(2)
+        for a in range(PASSES):
+            load_w(1, a, late=True)
 
         gather_words(0)
         quantize_w(0, 0)

from contextlib import ExitStack

import concourse.mybir as mybir
from concourse.masks import make_identity

K, M, T, S = 3072, 1024, 2048, 1024
FLOPS = 2 * K * M * S

F32 = mybir.dt.float32
BF16 = mybir.dt.bfloat16
I32 = mybir.dt.int32
U32 = mybir.dt.uint32
U16 = mybir.dt.uint16
U8 = mybir.dt.uint8
FP8X4 = mybir.dt.float8_e4m3fn_x4
FP4X4 = mybir.dt.float4_e2m1fn_x4
GELU = mybir.ActivationFunctionType.Gelu_apprx_tanh
ADD = mybir.AluOpType.add

P = 128
PACK = 4
K_PASS = P * PACK
PASSES = K // K_PASS
PAIRS = PASSES // 2
BLOCKS = K_PASS // 32
N_TILE = 512
TILES = S // P
WORD_BYTES = P * T * 4
SLOT = 4 * PACK * N_TILE
LATE_LOADS = 10

SCALAR_COLS = ((512, 512, 512, 384, 512, 320), (256, 512, 384, 128, 128, 192))
FIRST_HELD_BANK = 6
QUANTIZE_AFTER_ADD = {3: 0, FIRST_HELD_BANK - 1: 1}
BANK_BYTES = 4 * N_TILE
HELD_AT = LATE_LOADS * SLOT


def tile_list_tab4_tm_gelu_kernel(tc, tab, w, b, offs, out):
    nc = tc.nc
    with ExitStack() as ctx:
        keep = ctx.enter_context(tc.tile_pool(name="keep", bufs=1))
        ring = ctx.enter_context(tc.tile_pool(name="ring", bufs=2))
        placed = ctx.enter_context(tc.tile_pool(name="placed", bufs=1))
        psum = ctx.enter_context(tc.psum_pool(name="psum", bufs=1))

        slot_of = {}
        word_window = {}
        raw = {}
        parted = {}
        codes = {}
        w_plane = {}
        acc = {}
        summed = {}

        def landing(shape, dtype, name, late):
            if not late:
                return keep.tile(shape, dtype, name=name, align_bytes=64)
            slot_of[name] = len(slot_of)
            return placed.tile(shape, dtype, name=name, align_bytes=64, offset=SLOT * slot_of[name])

        def load_words(m, late):
            window = landing([P, T], U32, "word_window%d" % m, late)
            nc.sync.dma_start(
                out=window[:].bitcast(I32),
                in_=tab[m, 0:WORD_BYTES].rearrange("(p c) -> p c", p=P).bitcast(I32),
            )
            word_window[m] = window

        def load_w(half, a, late):
            rows = w[a * K_PASS : (a + 1) * K_PASS, half * N_TILE : (half + 1) * N_TILE]
            tile = landing([P, PACK, N_TILE], F32, "raw%d_%d" % (half, a), late)
            nc.sync.dma_start(out=tile[:], in_=rows.rearrange("(p j) n -> p j n", j=PACK))
            raw[half, a] = tile

        def move_scales(m):
            rows = picked_scales[:].rearrange("p h j -> p (h j)").bitcast(I32)
            planes = table_planes[:, 2 * m : 2 * m + 2, :].rearrange("p h j -> p (h j)")
            for r in range(4):
                nc.sync.dma_start(out=planes[r:P:32, :], in_=rows[4 * r + m : 4 * BLOCKS : 16, :])

        def gather_words(m):
            picked = ring.tile([P, S], U32, name="picked", align_bytes=64)
            nc.vector.tensor_copy(picked[:], word_window[m][:].indirect(offsets[:]))
            tile = keep.tile([P, 2, 2 * S], U8, name="parted%d" % m, align_bytes=64)
            nc.vector.tensor_copy(
                out=tile[:].bitcast(U16),
                in_=picked[:].bitcast(U16).rearrange("p (j h) -> p h j", h=2),
            )
            parted[m] = tile

        def quantize_w(half, a):
            if (half, a) == (1, 1):
                grouped = placed.tile([P, N_TILE, PACK], BF16, name="grouped_held", align_bytes=64, offset=HELD_AT)
            else:
                grouped = ring.tile([P, N_TILE, PACK], BF16, name="grouped", align_bytes=64)
            split = SCALAR_COLS[half][a]
            for copy, cols in ((nc.scalar.copy, slice(0, split)), (nc.vector.tensor_copy, slice(split, N_TILE))):
                if cols.start < cols.stop:
                    copy(
                        out=grouped[:, cols, :].rearrange("p (c i) t -> p c t i", i=4),
                        in_=raw[half, a][:, :, cols].rearrange("p t (c i) -> p c t i", i=4),
                    )
            code = keep.tile([P, N_TILE], U32, name="codes%d_%d" % (half, a), align_bytes=64)
            plane = keep.tile([P, N_TILE], U8, name="w_plane%d_%d" % (half, a), align_bytes=64)
            nc.vector.quantize_mx(
                out=code[:].bitcast(FP8X4), scales=plane[:], in_=grouped[:].rearrange("p n t -> p (n t)")
            )
            codes[half, a] = code
            w_plane[half, a] = plane

        def multiply(half, a, i, stop=False):
            start = (half, i) not in acc
            if start:
                acc[half, i] = psum.tile([P, N_TILE], F32, name="bank%d" % i)
            m, h = divmod(a, 2)
            nc.tensor.matmul_mx(
                out=acc[half, i][:],
                lhsT=parted[m][:, h, 2 * P * i : 2 * P * (i + 1)].bitcast(FP4X4),
                lhsT_scale=table_planes[:, a, :].bitcast(U8)[:, P * i : P * (i + 1)],
                rhs=codes[half, a][:].bitcast(FP8X4),
                rhs_scale=w_plane[half, a][:],
                start=start,
                stop=stop,
            )

        def add_bias(half, i, cols):
            if half == 0 and i >= FIRST_HELD_BANK:
                at = HELD_AT + BANK_BYTES * (i - FIRST_HELD_BANK)
                summed[half, i] = placed.tile([P, N_TILE], F32, name="held%d" % i, align_bytes=64, offset=at)
            elif (half, i) not in summed:
                summed[half, i] = keep.tile([P, N_TILE], F32, name="summed%d_%d" % (half, i))
            nc.vector.tensor_tensor(
                out=summed[half, i][:, cols],
                in0=acc[half, i][:, cols],
                in1=bias_row[:, half * N_TILE : (half + 1) * N_TILE][:, cols],
                op=ADD,
            )

        def activate_and_store(half, i, cols, result):
            nc.scalar.activation(out=result[:, cols], in_=summed[half, i][:, cols], func=GELU)
            rows = out[P * i : P * (i + 1), half * N_TILE : (half + 1) * N_TILE]
            nc.sync.dma_start(out=rows[:, cols], in_=result[:, cols])

        whole = slice(0, N_TILE)

        offsets = keep.tile([P, S // 16], U16, name="offsets")
        nc.sync.dma_start(offsets[:], offs)
        span = placed.tile([P, LATE_LOADS * SLOT // 4], I32, name="span", align_bytes=64, offset=0)
        scale_windows = span[:, 0 : 2 * T // 4].rearrange("p (h t) -> p h t", h=2)
        nc.vector.memset(scale_windows[4 * BLOCKS : P, :, :], 0)
        for place in range(4):
            scale_rows = tab[place % PAIRS, WORD_BYTES : WORD_BYTES + 2 * BLOCKS * T]
            nc.sync.dma_start(
                out=scale_windows[place : 4 * BLOCKS : 4, :, :],
                in_=scale_rows.rearrange("(h q t) -> q h t", h=2, q=BLOCKS).bitcast(I32),
            )
        load_words(0, late=False)
        b_rows = keep.tile([P, M // P], F32, name="b_rows")
        nc.sync.dma_start(out=b_rows[:], in_=b.rearrange("(p c) -> p c", p=P))
        load_w(0, 0, late=False)
        load_w(0, 1, late=False)
        load_words(1, late=False)
        load_w(0, 2, late=False)

        table_planes = keep.tile([P, PASSES, S // 4], I32, name="table_planes", align_bytes=64)
        nc.vector.memset(table_planes[:], 0)
        warm = keep.tile([P, 1], F32, name="warm")
        nc.vector.memset(warm[:], 0.0)
        nc.scalar.activation(out=warm[:], in_=warm[:], func=GELU)

        picked_scales = keep.tile([P, 2, S], U8, name="picked_scales", align_bytes=64)
        for h in range(2):
            nc.vector.tensor_copy(picked_scales[:, h, :], scale_windows[:, h, :].bitcast(U8).indirect(offsets[:]))
        move_scales(0)
        load_w(0, 3, late=True)
        load_words(2, late=True)
        move_scales(1)
        load_w(0, 4, late=True)
        load_w(0, 5, late=True)
        move_scales(2)
        for a in range(PASSES):
            load_w(1, a, late=True)

        gather_words(0)
        quantize_w(0, 0)

        ident = keep.tile([P, P], F32, name="ident")
        make_identity(nc, ident[:])
        bias = keep.tile([P, P, M // P], F32, name="bias")
        for g in range(2):
            spread = psum.tile([P, 4, P], F32, name="bank%d" % (TILES - 2 + g))
            for c in range(4):
                column = b_rows[:, 4 * g + c : 4 * g + c + 1]
                nc.tensor.transpose(spread[:, c, :], column.to_broadcast([P, P]), ident[:])
            nc.scalar.copy(out=bias[:, :, 4 * g : 4 * g + 4], in_=spread[:].rearrange("q c p -> q p c"))
        bias_row = bias[:].rearrange("q p c -> q (p c)")

        for a in range(PASSES):
            if a in (1, 3):
                gather_words((a + 1) // 2)
            if a > 0:
                quantize_w(0, a)
            for i in range(TILES):
                multiply(0, a, i, stop=(a == PASSES - 1))

        for i in range(TILES):
            add_bias(0, i, whole)
            if i in QUANTIZE_AFTER_ADD:
                quantize_w(1, QUANTIZE_AFTER_ADD[i])
        for a in (0, 1):
            for i in range(FIRST_HELD_BANK):
                multiply(1, a, i)
        for i in range(FIRST_HELD_BANK, TILES):
            multiply(1, 1, i)
            multiply(1, 0, i)
        for a in range(2, PASSES):
            quantize_w(1, a)
            if a < PASSES - 1:
                for i in range(TILES if a < PASSES - 2 else TILES // 2):
                    multiply(1, a, i)

        for i in range(TILES):
            at = SLOT * slot_of["raw1_%d" % (1 + i // 4)] + BANK_BYTES * (i % 4)
            result = placed.tile([P, N_TILE], F32, name="result%d" % i, align_bytes=64, offset=at)
            activate_and_store(0, i, whole, result)

        for i in range(TILES // 2):
            upper = i + TILES // 2
            multiply(1, PASSES - 1, i, stop=True)
            multiply(1, PASSES - 1, upper)
            multiply(1, PASSES - 2, upper, stop=True)
            for done in (i, upper):
                pieces = [whole] if done < TILES - 1 else [slice(0, N_TILE // 2), slice(N_TILE // 2, N_TILE)]
                for cols in pieces:
                    add_bias(1, done, cols)
                    activate_and_store(1, done, cols, summed[1, done])
